import numpy as np
import ml_dtypes


def mxq(x, axis, fmt="e4m3"):
    dtype, down = {"e4m3": (ml_dtypes.float8_e4m3fn, 7), "e5m2": (ml_dtypes.float8_e5m2, 14)}[fmt]
    v = np.moveaxis(np.asarray(x, np.float32).astype(ml_dtypes.bfloat16).astype(np.float64), axis, -1)
    blocks = v.reshape(v.shape[:-1] + (-1, 32))
    amax = np.abs(blocks).max(-1, keepdims=True)
    byte = np.maximum(np.where(amax > 0, np.frexp(amax)[1] - 1 + 127, 0) - down, 1)
    scale = np.exp2(byte - 127.0)
    codes = (blocks / scale).astype(np.float32).astype(dtype).astype(np.float64)
    return np.moveaxis((codes * scale).reshape(v.shape), -1, axis)


WIDE = False


def mx_kscale(k):
    if not WIDE:
        return np.ones(k)
    levels = np.array([10, -10, 5, -5, 0])
    if k % 512:
        return np.exp2(np.random.permutation(np.resize(levels, k // 32))).repeat(32)
    a = np.empty((k // 512, 16))
    for p in range(k // 512):
        a[p, :8] = np.random.permutation(np.resize(levels, 8))
        for g in range(8):
            far = levels[np.abs(levels - a[p, g]) >= 10]
            a[p, g + 8] = far[np.random.randint(len(far))]
    return np.exp2(a.ravel()).repeat(32)


BF16 = ml_dtypes.bfloat16


def bf(x):
    return np.asarray(x, np.float32).astype(BF16)


def f64(x):
    return np.asarray(x).astype(np.float64)


E2M1 = np.array([0.0, 0.5, 1.0, 1.5, 2.0, 3.0, 4.0, 6.0, -0.0, -0.5, -1.0, -1.5, -2.0, -3.0, -4.0, -6.0])


def pack_weight(w, fmt):
    k, n = w.shape
    w = f64(bf(w)).reshape(k // 32, 32, n)
    amax = np.abs(w).max(1)
    if fmt == "e4m3":
        byte = np.frexp(amax)[1] - 1 + 127 - 7
    else:
        mant, ex = np.frexp(amax / 6.0)
        byte = np.where(mant > 0.5, ex, ex - 1) + 127
    byte = np.clip(np.where(amax > 0, byte, 1), 1, 254)
    scaled = (w * np.exp2(127.0 - byte)[:, None, :]).reshape(k, n).astype(np.float32)
    by_word = np.ascontiguousarray(scaled.reshape(k // 512, 128, 4, n).transpose(0, 1, 3, 2))
    if fmt == "e4m3":
        words = by_word.astype(ml_dtypes.float8_e4m3fn).view(np.uint8)
    else:
        c = by_word.astype(ml_dtypes.float4_e2m1fn).view(np.uint8) & 0xF
        words = c[..., 0::2] | (c[..., 1::2] << 4)
    return np.ascontiguousarray(words), np.ascontiguousarray(byte.astype(np.uint8).reshape(k // 512, 16, n))


def unpack_weight(words, scales, fmt):
    g, p, n, _ = words.shape
    if fmt == "e4m3":
        vals = np.ascontiguousarray(words).view(ml_dtypes.float8_e4m3fn).astype(np.float64)
    else:
        nib = np.empty((g, p, n, 4), np.uint8)
        nib[..., 0::2] = words & 0xF
        nib[..., 1::2] = words >> 4
        vals = E2M1[nib]
    vals = vals * np.repeat(np.exp2(scales.astype(np.float64) - 127.0), 8, axis=1)[..., None]
    return vals.transpose(0, 1, 3, 2).reshape(g * 512, n)
def pack4(w):
    words, scales = pack_weight(w, "e2m1")
    return words.reshape(words.shape[0], 128, -1), scales


def unpack4(words, scales):
    return unpack_weight(words.reshape(words.shape[0], 128, -1, 2), scales, "e2m1")


S, F, N = 2048, 1536, 512


def setup_inputs():
    s = mx_kscale(S)
    acts = np.random.standard_normal((S, F)) * s[:, None]
    e_real = np.random.standard_normal((S, N)) / np.sqrt(S) / s[:, None]
    e_anchor = np.random.standard_normal((S, N)) / np.sqrt(S) / s[:, None]
    e_syn = np.random.standard_normal((S, N)) / np.sqrt(S) / s[:, None]
    real_words, real_scales = pack4(e_real)
    anchor_words, anchor_scales = pack_weight(e_anchor, "e4m3")
    return {"acts": bf(acts),
            "real_words": real_words, "real_scales": real_scales,
            "anchor_words": anchor_words, "anchor_scales": anchor_scales,
            "e_syn": bf(e_syn),
            "damp": bf(1.0 + 0.5 * np.random.random(N))}


def reference(acts, real_words, real_scales, anchor_words, anchor_scales, e_syn, damp):
    a = mxq(f64(acts), 0, "e4m3")
    g_real = a.T @ unpack4(real_words, real_scales)
    g_anchor = a.T @ unpack_weight(anchor_words, anchor_scales, "e4m3")
    g_syn = a.T @ mxq(f64(e_syn), 0, "e4m3")
    return (g_real - g_syn) / (f64(damp) + np.abs(g_anchor))

@@ -1,0 +1,274 @@
+from contextlib import ExitStack
+
+import concourse.mybir as mybir
+
+S, F, N = 2048, 1536, 512
+FLOPS = 3 * 2 * S * F * N
+
+F32 = mybir.dt.float32
+BF16 = mybir.dt.bfloat16
+U32 = mybir.dt.uint32
+I32 = mybir.dt.int32
+U8 = mybir.dt.uint8
+FP8X4 = mybir.dt.float8_e4m3fn_x4
+FP4X4 = mybir.dt.float4_e2m1fn_x4
+ALU = mybir.AluOpType
+ACT = mybir.ActivationFunctionType
+
+P = 128
+PACK = 4
+GROUPS = S // (P * PACK)
+TILES = F // P
+FIRST = 4
+LOAD_BLOCKS = [(4, 6), (6, 8), (8, 12)]
+SYN_V = 288
+SP = 0
+ORDER = "p4 a4 r0 r1 d4 p5 a5 r2 p6 d5 a6 r3 p7 d6 a7 r4 p8 d7 a8 r5 p9 d8 a9 r6 p10 r7 d9 a10 p11 r8 a11 d10 r9 r10 d11 r11 r12"
+
+
+def tile_label_distillation_discrepancy_s10_kernel(
+    tc, acts, real_words, real_scales, anchor_words, anchor_scales, e_syn, damp, out
+):
+    nc = tc.nc
+    with ExitStack() as ctx:
+        keep = ctx.enter_context(tc.tile_pool(name="keep", bufs=1))
+        stage = ctx.enter_context(tc.tile_pool(name="stage", bufs=1))
+        psum = ctx.enter_context(tc.psum_pool(name="psum", bufs=1))
+        ctx.enter_context(tc.manual_schedule())
+
+        a_rows = {}
+        syn_rows, anchor_codes, real_codes = {}, {}, {}
+
+        def load_a(g, m0, m1):
+            rows = keep.tile([P, PACK, (m1 - m0) * P], BF16, name="a_rows_%d_%d" % (g, m0))
+            src = acts[g * P * PACK : (g + 1) * P * PACK, m0 * P : m1 * P]
+            nc.sync.dma_start(out=rows[:], in_=src.rearrange("(p t) c -> p t c", t=PACK))
+            for m in range(m0, m1):
+                a_rows[g, m] = rows[:, :, (m - m0) * P : (m - m0 + 1) * P]
+
+        def load_syn(g):
+            rows = keep.tile([P, PACK, N], BF16, name="syn_rows_%d" % g)
+            src = e_syn[g * P * PACK : (g + 1) * P * PACK, :]
+            nc.sync.dma_start(out=rows[:], in_=src.rearrange("(p t) c -> p t c", t=PACK))
+            syn_rows[g] = rows
+
+        def load_anchor(g):
+            codes = keep.tile([P, N], U32, name="anchor_codes_%d" % g, align_bytes=64)
+            nc.sync.dma_start(
+                out=codes[:].bitcast(I32), in_=anchor_words[g].rearrange("p n t -> p (n t)").bitcast(I32)
+            )
+            anchor_codes[g] = codes
+
+        def load_real(g):
+            codes = keep.tile([P, 2 * N], U8, name="real_codes_%d" % g, align_bytes=64)
+            nc.sync.dma_start(out=codes[:].bitcast(I32), in_=real_words[g].bitcast(I32))
+            real_codes[g] = codes
+
+        def load_scales(queue, plane, scales):
+            for q in range(4):
+                queue.dma_start(
+                    out=plane[32 * q : 32 * q + 4].bitcast(I32),
+                    in_=scales[:, 4 * q : 4 * q + 4, :].rearrange("g r n -> r g n").bitcast(I32),
+                )
+
+        anchor_plane = keep.tile([P, GROUPS, N], U8, name="anchor_plane", align_bytes=64)
+        real_plane = keep.tile([P, GROUPS, N], U8, name="real_plane", align_bytes=64)
+        nc.vector.memset(anchor_plane[:].bitcast(I32), 0)
+        nc.vector.memset(real_plane[:].bitcast(I32), 0)
+
+        damp_rows = keep.tile([P, N], BF16, name="damp_rows", align_bytes=64)
+        nc.vector.memset(damp_rows[:].bitcast(I32), 0)
+        nc.gpsimd.dma_start(out=damp_rows[0:P:32, :], in_=damp.partition_broadcast(4))
+
+        load_a(0, 0, 2)
+        load_anchor(0)
+        load_scales(nc.scalar, anchor_plane, anchor_scales)
+        load_a(0, 2, FIRST)
+        load_real(0)
+        load_a(1, 0, FIRST)
+        load_anchor(1)
+        load_scales(nc.sync, real_plane, real_scales)
+        load_real(1)
+        for g in range(2, GROUPS):
+            load_syn(g - 2)
+            load_a(g, 0, FIRST)
+            load_anchor(g)
+            load_real(g)
+        load_syn(GROUPS - 2)
+        load_syn(GROUPS - 1)
+        for m0, m1 in LOAD_BLOCKS:
+            for g in range(GROUPS):
+                load_a(g, m0, m1)
+
+        def interleave_views(words, rows):
+            return (
+                words.rearrange("p (c i) t -> p c t i", i=4),
+                rows.rearrange("p t (c i) -> p c t i", i=4),
+            )
+
+        a_words, a_codes, a_scales = {}, {}, {}
+
+        def interleave_a(engine, g, m):
+            words = stage.tile([P, P, PACK], BF16, name="a_words", bufs=8, align_bytes=64)
+            dst, src = interleave_views(words[:], a_rows[g, m])
+            if engine is nc.vector:
+                nc.vector.tensor_copy(out=dst, in_=src)
+            else:
+                nc.scalar.copy(out=dst, in_=src)
+            a_words[g, m] = words
+
+        def quantize_a(g, m):
+            codes = keep.tile([P, P], U32, name="a_codes_%d_%d" % (g, m), align_bytes=64)
+            scales = keep.tile([P, P], U8, name="a_scales_%d_%d" % (g, m), align_bytes=64)
+            nc.vector.quantize_mx(
+                out=codes[:].bitcast(FP8X4), scales=scales[:], in_=a_words[g, m][:].rearrange("p c t -> p (c t)")
+            )
+            a_codes[g, m], a_scales[g, m] = codes, scales
+
+        syn_words, syn_codes, syn_scales = {}, {}, {}
+
+        def interleave_syn(g):
+            words = stage.tile([P, N, PACK], BF16, name="syn_words", bufs=2, align_bytes=64)
+            dst, src = interleave_views(words[:, SYN_V:, :], syn_rows[g][:, :, SYN_V:])
+            nc.scalar.activation(out=dst, in_=src, func=ACT.Copy, scale=-1.0)
+            dst, src = interleave_views(words[:, :SYN_V, :], syn_rows[g][:, :, :SYN_V])
+            nc.vector.tensor_scalar(out=dst, in0=src, scalar1=-1.0, scalar2=None, op0=ALU.mult)
+            syn_words[g] = words
+
+        def quantize_syn(g):
+            codes = keep.tile([P, N], U32, name="syn_codes_%d" % g, align_bytes=64)
+            scales = keep.tile([P, N], U8, name="syn_scales_%d" % g, align_bytes=64)
+            nc.vector.quantize_mx(
+                out=codes[:].bitcast(FP8X4), scales=scales[:], in_=syn_words[g][:].rearrange("p c t -> p (c t)")
+            )
+            syn_codes[g], syn_scales[g] = codes, scales
+
+        anchor_bank, diff_bank, divisor = {}, {}, {}
+
+        def mx_pass(bank, g, m, codes, scales, start, stop):
+            nc.tensor.matmul_mx(
+                out=bank[:],
+                lhsT=a_codes[g, m][:].bitcast(FP8X4),
+                lhsT_scale=a_scales[g, m][:],
+                rhs=codes,
+                rhs_scale=scales,
+                start=start,
+                stop=stop,
+            )
+
+        def anchor_pass(g, m):
+            if g == 0:
+                anchor_bank[m] = psum.tile([P, N], F32, name="anchor_bank_%d" % (m % FIRST))
+            mx_pass(
+                anchor_bank[m], g, m, anchor_codes[g][:].bitcast(FP8X4), anchor_plane[:, g, :], g == 0, g == GROUPS - 1
+            )
+
+        def real_pass(g, m):
+            if g == 0:
+                diff_bank[m] = psum.tile([P, N], F32, name="diff_bank_%d" % (m % FIRST))
+            mx_pass(diff_bank[m], g, m, real_codes[g][:].bitcast(FP4X4), real_plane[:, g, :], g == 0, False)
+
+        def syn_pass(g, m):
+            mx_pass(diff_bank[m], g, m, syn_codes[g][:].bitcast(FP8X4), syn_scales[g][:], False, g == GROUPS - 1)
+
+        def take_abs(m):
+            divisor[m] = stage.tile([P, N], F32, name="divisor", bufs=6)
+            nc.scalar.activation(out=divisor[m][:], in_=anchor_bank[m][:], func=ACT.Abs)
+
+        def add_damp(m):
+            nc.vector.tensor_tensor(out=divisor[m][:], in0=divisor[m][:], in1=damp_all[:], op=ALU.add)
+
+        def inverse_root(m):
+            nc.scalar.activation(out=divisor[m][:], in_=divisor[m][:], func=ACT.Abs_reciprocal_sqrt)
+
+        def square(m):
+            nc.scalar.activation(out=divisor[m][:], in_=divisor[m][:], func=ACT.Square)
+
+        def finish(m):
+            result = stage.tile([P, N], F32, name="result", bufs=6)
+            nc.vector.tensor_tensor(out=result[:], in0=diff_bank[m][:], in1=divisor[m][:], op=ALU.mult)
+            nc.sync.dma_start(out=out[m * P : (m + 1) * P, :], in_=result[:])
+
+        damp_all = keep.tile([P, N], BF16, name="damp_all", align_bytes=64)
+
+        turned = keep.tile([P, N], BF16, name="damp_turned", align_bytes=64)
+        filled = keep.tile([P, N], BF16, name="damp_filled", align_bytes=64)
+
+        for g in range(GROUPS):
+            if g == 0:
+                for m in (0, 2):
+                    interleave_a(nc.vector, g, m)
+                    interleave_a(nc.scalar, g, m + 1)
+                    quantize_a(g, m)
+                    quantize_a(g, m + 1)
+                    if m == 0:
+                        nc.vector.transpose(turned[:], damp_rows[:])
+                nc.vector.tensor_copy(
+                    out=filled[:].rearrange("p (b j) -> p b j", j=32),
+                    in_=turned[:].rearrange("p (b j) -> p b j", j=32)[:, :, 0:1].to_broadcast([P, N // 32, 32]),
+                )
+            else:
+                for m in (0, 2):
+                    interleave_a(nc.vector, g, m)
+                    interleave_a(nc.scalar, g, m + 1)
+                for m in range(FIRST):
+                    quantize_a(g, m)
+            for m in range(FIRST):
+                anchor_pass(g, m)
+            for m in range(FIRST):
+                real_pass(g, m)
+            if g == 1:
+                nc.vector.transpose(damp_all[:], filled[:])
+            if g > 0:
+                interleave_syn(g - 1)
+                quantize_syn(g - 1)
+                for m in range(FIRST):
+                    syn_pass(g - 1, m)
+        interleave_syn(GROUPS - 1)
+        take_abs(0)
+        quantize_syn(GROUPS - 1)
+        add_damp(0)
+        take_abs(1)
+        for m in range(FIRST):
+            syn_pass(GROUPS - 1, m)
+
+        def prepare(m):
+            interleave_a(nc.scalar, 0, m)
+            interleave_a(nc.vector, 1, m)
+            interleave_a(nc.vector if m % 2 == SP else nc.scalar, 3, m)
+            interleave_a(nc.vector, 2, m)
+            for g in range(GROUPS):
+                quantize_a(g, m)
+
+        def anchor_passes(m):
+            for g in range(GROUPS):
+                anchor_pass(g, m)
+
+        def diff_passes(m):
+            for g in range(GROUPS):
+                real_pass(g, m)
+            for g in range(GROUPS):
+                syn_pass(g, m)
+
+        def epilogue_round(r):
+            if r < TILES:
+                inverse_root(r)
+            if r + 2 < TILES:
+                take_abs(r + 2)
+            if r < TILES:
+                square(r)
+            if r > 0:
+                finish(r - 1)
+            if r + 1 < TILES:
+                add_damp(r + 1)
+
+        for step in ORDER.split():
+            kind, m = step[0], int(step[1:])
+            if kind == "p":
+                prepare(m)
+            if kind == "a":
+                anchor_passes(m)
+            if kind == "d":
+                diff_passes(m)
+            if kind == "r":
+                epilogue_round(m)

@@ -17,13 +17,19 @@ ACT = mybir.ActivationFunctionType
 
 P = 128
 PACK = 4
+QUADRANT = 32
+SCALE_ROWS = 4
 GROUPS = S // (P * PACK)
 TILES = F // P
-FIRST = 4
-LOAD_BLOCKS = [(4, 6), (6, 8), (8, 12)]
-SYN_V = 288
-SP = 0
-ORDER = "p4 a4 r0 r1 d4 p5 a5 r2 p6 d5 a6 r3 p7 d6 a7 r4 p8 d7 a8 r5 p9 d8 a9 r6 p10 r7 d9 a10 p11 r8 a11 d10 r9 r10 d11 r11 r12"
+BANKS = 8
+FIRST_TILES = BANKS // 2
+PAIR = 2
+RUN = 4
+SYN_VECTOR_COLUMNS = 320
+ANCHOR_AHEAD_FROM = TILES - 2
+WORD_BUFS = 8
+DIVISOR_BUFS = 6
+RESULT_BUFS = 6
 
 
 def tile_label_distillation_discrepancy_s10_kernel(
@@ -36,27 +42,26 @@ def tile_label_distillation_discrepancy_s10_kernel(
         psum = ctx.enter_context(tc.psum_pool(name="psum", bufs=1))
         ctx.enter_context(tc.manual_schedule())
 
-        a_rows = {}
-        syn_rows, anchor_codes, real_codes = {}, {}, {}
+        a_rows, syn_rows, anchor_codes, real_codes = {}, {}, {}, {}
+
+        def load_rows(name, matrix, g, c0, c1):
+            rows = keep.tile([P, PACK, c1 - c0], BF16, name=name)
+            src = matrix[g * P * PACK : (g + 1) * P * PACK, c0:c1]
+            nc.sync.dma_start(out=rows[:], in_=src.rearrange("(p t) c -> p t c", t=PACK))
+            return rows
 
         def load_a(g, m0, m1):
-            rows = keep.tile([P, PACK, (m1 - m0) * P], BF16, name="a_rows_%d_%d" % (g, m0))
-            src = acts[g * P * PACK : (g + 1) * P * PACK, m0 * P : m1 * P]
-            nc.sync.dma_start(out=rows[:], in_=src.rearrange("(p t) c -> p t c", t=PACK))
+            rows = load_rows("a_rows_%d_%d" % (g, m0), acts, g, m0 * P, m1 * P)
             for m in range(m0, m1):
                 a_rows[g, m] = rows[:, :, (m - m0) * P : (m - m0 + 1) * P]
 
         def load_syn(g):
-            rows = keep.tile([P, PACK, N], BF16, name="syn_rows_%d" % g)
-            src = e_syn[g * P * PACK : (g + 1) * P * PACK, :]
-            nc.sync.dma_start(out=rows[:], in_=src.rearrange("(p t) c -> p t c", t=PACK))
-            syn_rows[g] = rows
+            syn_rows[g] = load_rows("syn_rows_%d" % g, e_syn, g, 0, N)
 
         def load_anchor(g):
             codes = keep.tile([P, N], U32, name="anchor_codes_%d" % g, align_bytes=64)
-            nc.sync.dma_start(
-                out=codes[:].bitcast(I32), in_=anchor_words[g].rearrange("p n t -> p (n t)").bitcast(I32)
-            )
+            src = anchor_words[g].rearrange("p n t -> p (n t)")
+            nc.sync.dma_start(out=codes[:].bitcast(I32), in_=src.bitcast(I32))
             anchor_codes[g] = codes
 
         def load_real(g):
@@ -64,57 +69,60 @@ def tile_label_distillation_discrepancy_s10_kernel(
             nc.sync.dma_start(out=codes[:].bitcast(I32), in_=real_words[g].bitcast(I32))
             real_codes[g] = codes
 
-        def load_scales(queue, plane, scales):
-            for q in range(4):
-                queue.dma_start(
-                    out=plane[32 * q : 32 * q + 4].bitcast(I32),
-                    in_=scales[:, 4 * q : 4 * q + 4, :].rearrange("g r n -> r g n").bitcast(I32),
-                )
+        damp_rows = keep.tile([P, N], BF16, name="damp_rows", align_bytes=64)
+        nc.vector.memset(damp_rows[:].bitcast(I32), 0)
+        nc.scalar.dma_start(out=damp_rows[0:P:QUADRANT, :], in_=damp.partition_broadcast(P // QUADRANT))
 
-        anchor_plane = keep.tile([P, GROUPS, N], U8, name="anchor_plane", align_bytes=64)
+        anchor_plane = keep.tile([P, N], U8, name="anchor_plane", align_bytes=64)
         real_plane = keep.tile([P, GROUPS, N], U8, name="real_plane", align_bytes=64)
         nc.vector.memset(anchor_plane[:].bitcast(I32), 0)
         nc.vector.memset(real_plane[:].bitcast(I32), 0)
 
-        damp_rows = keep.tile([P, N], BF16, name="damp_rows", align_bytes=64)
-        nc.vector.memset(damp_rows[:].bitcast(I32), 0)
-        nc.gpsimd.dma_start(out=damp_rows[0:P:32, :], in_=damp.partition_broadcast(4))
+        def load_anchor_scales():
+            for q in range(P // QUADRANT):
+                nc.sync.dma_start(
+                    out=anchor_plane[QUADRANT * q : QUADRANT * q + GROUPS * SCALE_ROWS, :].bitcast(I32),
+                    in_=anchor_scales[:, SCALE_ROWS * q : SCALE_ROWS * (q + 1), :].bitcast(I32),
+                )
 
-        load_a(0, 0, 2)
+        def load_real_scales():
+            for q in range(P // QUADRANT):
+                src = real_scales[:, SCALE_ROWS * q : SCALE_ROWS * (q + 1), :].rearrange("g r n -> r g n")
+                nc.sync.dma_start(
+                    out=real_plane[QUADRANT * q : QUADRANT * q + SCALE_ROWS].bitcast(I32), in_=src.bitcast(I32)
+                )
+
+        table_preload = keep.tile([P, 1], F32, name="table_preload")
+        nc.vector.memset(table_preload[:], 1.0)
+        nc.scalar.activation(out=table_preload[:], in_=table_preload[:], func=ACT.Abs_reciprocal_sqrt)
+
+        load_a(0, 0, FIRST_TILES)
+        load_anchor_scales()
         load_anchor(0)
-        load_scales(nc.scalar, anchor_plane, anchor_scales)
-        load_a(0, 2, FIRST)
         load_real(0)
-        load_a(1, 0, FIRST)
-        load_anchor(1)
-        load_scales(nc.sync, real_plane, real_scales)
-        load_real(1)
-        for g in range(2, GROUPS):
-            load_syn(g - 2)
-            load_a(g, 0, FIRST)
+        load_syn(0)
+        load_real_scales()
+        for g in range(1, GROUPS):
+            load_a(g, 0, FIRST_TILES)
             load_anchor(g)
+            load_syn(g)
             load_real(g)
-        load_syn(GROUPS - 2)
-        load_syn(GROUPS - 1)
-        for m0, m1 in LOAD_BLOCKS:
+        for m in range(FIRST_TILES, TILES, PAIR):
             for g in range(GROUPS):
-                load_a(g, m0, m1)
+                load_a(g, m, m + PAIR)
 
         def interleave_views(words, rows):
             return (
-                words.rearrange("p (c i) t -> p c t i", i=4),
-                rows.rearrange("p t (c i) -> p c t i", i=4),
+                words.rearrange("p (c i) t -> p c t i", i=RUN),
+                rows.rearrange("p t (c i) -> p c t i", i=RUN),
             )
 
         a_words, a_codes, a_scales = {}, {}, {}
 
-        def interleave_a(engine, g, m):
-            words = stage.tile([P, P, PACK], BF16, name="a_words", bufs=8, align_bytes=64)
+        def interleave_a(copy, g, m):
+            words = stage.tile([P, P, PACK], BF16, name="a_words", bufs=WORD_BUFS, align_bytes=64)
             dst, src = interleave_views(words[:], a_rows[g, m])
-            if engine is nc.vector:
-                nc.vector.tensor_copy(out=dst, in_=src)
-            else:
-                nc.scalar.copy(out=dst, in_=src)
+            copy(out=dst, in_=src)
             a_words[g, m] = words
 
         def quantize_a(g, m):
@@ -125,29 +133,56 @@ def tile_label_distillation_discrepancy_s10_kernel(
             )
             a_codes[g, m], a_scales[g, m] = codes, scales
 
-        syn_words, syn_codes, syn_scales = {}, {}, {}
+        on_vector, on_scalar = nc.vector.tensor_copy, nc.scalar.copy
 
-        def interleave_syn(g):
+        def prepare_first_tiles(g):
+            for m in range(0, FIRST_TILES, 2):
+                interleave_a(on_vector, g, m)
+                interleave_a(on_scalar, g, m + 1)
+            for m in list(range(0, FIRST_TILES, 2)) + list(range(1, FIRST_TILES, 2)):
+                quantize_a(g, m)
+
+        def prepare_tile(m):
+            still_arriving = m == FIRST_TILES
+            interleave_a(on_scalar, 0, m)
+            interleave_a(on_vector, 1, m)
+            if m % 2 == 1:
+                interleave_a(on_scalar, 3, m)
+            if still_arriving:
+                quantize_a(0, m)
+            interleave_a(on_vector, 2, m)
+            if not still_arriving:
+                quantize_a(0, m)
+            quantize_a(1, m)
+            if m % 2 == 0:
+                interleave_a(on_vector, 3, m)
+            quantize_a(2, m)
+            quantize_a(3, m)
+
+        syn_codes, syn_scales = {}, {}
+
+        def prepare_syn(g):
             words = stage.tile([P, N, PACK], BF16, name="syn_words", bufs=2, align_bytes=64)
-            dst, src = interleave_views(words[:, SYN_V:, :], syn_rows[g][:, :, SYN_V:])
+            dst, src = interleave_views(words[:, SYN_VECTOR_COLUMNS:, :], syn_rows[g][:, :, SYN_VECTOR_COLUMNS:])
             nc.scalar.activation(out=dst, in_=src, func=ACT.Copy, scale=-1.0)
-            dst, src = interleave_views(words[:, :SYN_V, :], syn_rows[g][:, :, :SYN_V])
+            dst, src = interleave_views(words[:, :SYN_VECTOR_COLUMNS, :], syn_rows[g][:, :, :SYN_VECTOR_COLUMNS])
             nc.vector.tensor_scalar(out=dst, in0=src, scalar1=-1.0, scalar2=None, op0=ALU.mult)
-            syn_words[g] = words
-
-        def quantize_syn(g):
             codes = keep.tile([P, N], U32, name="syn_codes_%d" % g, align_bytes=64)
             scales = keep.tile([P, N], U8, name="syn_scales_%d" % g, align_bytes=64)
-            nc.vector.quantize_mx(
-                out=codes[:].bitcast(FP8X4), scales=scales[:], in_=syn_words[g][:].rearrange("p c t -> p (c t)")
-            )
+            for cols in (slice(0, N // 2), slice(N // 2, N)):
+                nc.vector.quantize_mx(
+                    out=codes[:, cols].bitcast(FP8X4),
+                    scales=scales[:, cols],
+                    in_=words[:, cols, :].rearrange("p c t -> p (c t)"),
+                )
             syn_codes[g], syn_scales[g] = codes, scales
 
-        anchor_bank, diff_bank, divisor = {}, {}, {}
+        free_banks = ["bank_%d" % b for b in range(BANKS)]
+        anchor_sum, anchor_bank, diff_sum, diff_bank = {}, {}, {}, {}
 
-        def mx_pass(bank, g, m, codes, scales, start, stop):
+        def mx_pass(acc, g, m, codes, scales, start, stop):
             nc.tensor.matmul_mx(
-                out=bank[:],
+                out=acc[:],
                 lhsT=a_codes[g, m][:].bitcast(FP8X4),
                 lhsT_scale=a_scales[g, m][:],
                 rhs=codes,
@@ -158,87 +193,19 @@ def tile_label_distillation_discrepancy_s10_kernel(
 
         def anchor_pass(g, m):
             if g == 0:
-                anchor_bank[m] = psum.tile([P, N], F32, name="anchor_bank_%d" % (m % FIRST))
-            mx_pass(
-                anchor_bank[m], g, m, anchor_codes[g][:].bitcast(FP8X4), anchor_plane[:, g, :], g == 0, g == GROUPS - 1
-            )
+                anchor_bank[m] = free_banks.pop(0)
+                anchor_sum[m] = psum.tile([P, N], F32, name=anchor_bank[m])
+            codes, scales = anchor_codes[g][:].bitcast(FP8X4), anchor_plane[SCALE_ROWS * g :, :]
+            mx_pass(anchor_sum[m], g, m, codes, scales, g == 0, g == GROUPS - 1)
 
         def real_pass(g, m):
             if g == 0:
-                diff_bank[m] = psum.tile([P, N], F32, name="diff_bank_%d" % (m % FIRST))
-            mx_pass(diff_bank[m], g, m, real_codes[g][:].bitcast(FP4X4), real_plane[:, g, :], g == 0, False)
+                diff_bank[m] = free_banks.pop(0)
+                diff_sum[m] = psum.tile([P, N], F32, name=diff_bank[m])
+            mx_pass(diff_sum[m], g, m, real_codes[g][:].bitcast(FP4X4), real_plane[:, g, :], g == 0, False)
 
         def syn_pass(g, m):
-            mx_pass(diff_bank[m], g, m, syn_codes[g][:].bitcast(FP8X4), syn_scales[g][:], False, g == GROUPS - 1)
-
-        def take_abs(m):
-            divisor[m] = stage.tile([P, N], F32, name="divisor", bufs=6)
-            nc.scalar.activation(out=divisor[m][:], in_=anchor_bank[m][:], func=ACT.Abs)
-
-        def add_damp(m):
-            nc.vector.tensor_tensor(out=divisor[m][:], in0=divisor[m][:], in1=damp_all[:], op=ALU.add)
-
-        def inverse_root(m):
-            nc.scalar.activation(out=divisor[m][:], in_=divisor[m][:], func=ACT.Abs_reciprocal_sqrt)
-
-        def square(m):
-            nc.scalar.activation(out=divisor[m][:], in_=divisor[m][:], func=ACT.Square)
-
-        def finish(m):
-            result = stage.tile([P, N], F32, name="result", bufs=6)
-            nc.vector.tensor_tensor(out=result[:], in0=diff_bank[m][:], in1=divisor[m][:], op=ALU.mult)
-            nc.sync.dma_start(out=out[m * P : (m + 1) * P, :], in_=result[:])
-
-        damp_all = keep.tile([P, N], BF16, name="damp_all", align_bytes=64)
-
-        turned = keep.tile([P, N], BF16, name="damp_turned", align_bytes=64)
-        filled = keep.tile([P, N], BF16, name="damp_filled", align_bytes=64)
-
-        for g in range(GROUPS):
-            if g == 0:
-                for m in (0, 2):
-                    interleave_a(nc.vector, g, m)
-                    interleave_a(nc.scalar, g, m + 1)
-                    quantize_a(g, m)
-                    quantize_a(g, m + 1)
-                    if m == 0:
-                        nc.vector.transpose(turned[:], damp_rows[:])
-                nc.vector.tensor_copy(
-                    out=filled[:].rearrange("p (b j) -> p b j", j=32),
-                    in_=turned[:].rearrange("p (b j) -> p b j", j=32)[:, :, 0:1].to_broadcast([P, N // 32, 32]),
-                )
-            else:
-                for m in (0, 2):
-                    interleave_a(nc.vector, g, m)
-                    interleave_a(nc.scalar, g, m + 1)
-                for m in range(FIRST):
-                    quantize_a(g, m)
-            for m in range(FIRST):
-                anchor_pass(g, m)
-            for m in range(FIRST):
-                real_pass(g, m)
-            if g == 1:
-                nc.vector.transpose(damp_all[:], filled[:])
-            if g > 0:
-                interleave_syn(g - 1)
-                quantize_syn(g - 1)
-                for m in range(FIRST):
-                    syn_pass(g - 1, m)
-        interleave_syn(GROUPS - 1)
-        take_abs(0)
-        quantize_syn(GROUPS - 1)
-        add_damp(0)
-        take_abs(1)
-        for m in range(FIRST):
-            syn_pass(GROUPS - 1, m)
-
-        def prepare(m):
-            interleave_a(nc.scalar, 0, m)
-            interleave_a(nc.vector, 1, m)
-            interleave_a(nc.vector if m % 2 == SP else nc.scalar, 3, m)
-            interleave_a(nc.vector, 2, m)
-            for g in range(GROUPS):
-                quantize_a(g, m)
+            mx_pass(diff_sum[m], g, m, syn_codes[g][:].bitcast(FP8X4), syn_scales[g][:], False, g == GROUPS - 1)
 
         def anchor_passes(m):
             for g in range(GROUPS):
@@ -250,6 +217,33 @@ def tile_label_distillation_discrepancy_s10_kernel(
             for g in range(GROUPS):
                 syn_pass(g, m)
 
+        divisor = {}
+
+        def take_abs(m):
+            divisor[m] = stage.tile([P, N], F32, name="divisor", bufs=DIVISOR_BUFS)
+            nc.scalar.activation(out=divisor[m][:], in_=anchor_sum[m][:], func=ACT.Abs)
+            free_banks.append(anchor_bank[m])
+
+        def add_damp(m):
+            nc.vector.tensor_tensor(out=divisor[m][:], in0=divisor[m][:], in1=damp_all[:], op=ALU.add)
+
+        def inverse_root(m):
+            nc.scalar.activation(out=divisor[m][:], in_=divisor[m][:], func=ACT.Abs_reciprocal_sqrt)
+
+        def square(m):
+            nc.scalar.activation(out=divisor[m][:], in_=divisor[m][:], func=ACT.Square)
+
+        def multiply_and_store(m):
+            result = stage.tile([P, N], F32, name="result", bufs=RESULT_BUFS)
+            pieces = 2 if m == TILES - 1 else 1
+            for h in range(pieces):
+                cols = slice(h * N // pieces, (h + 1) * N // pieces)
+                nc.vector.tensor_tensor(
+                    out=result[:, cols], in0=diff_sum[m][:, cols], in1=divisor[m][:, cols], op=ALU.mult
+                )
+                nc.sync.dma_start(out=out[m * P : (m + 1) * P, cols], in_=result[:, cols])
+            free_banks.append(diff_bank[m])
+
         def epilogue_round(r):
             if r < TILES:
                 inverse_root(r)
@@ -258,17 +252,49 @@ def tile_label_distillation_discrepancy_s10_kernel(
             if r < TILES:
                 square(r)
             if r > 0:
-                finish(r - 1)
+                multiply_and_store(r - 1)
             if r + 1 < TILES:
                 add_damp(r + 1)
 
-        for step in ORDER.split():
-            kind, m = step[0], int(step[1:])
-            if kind == "p":
-                prepare(m)
-            if kind == "a":
+        damp_turned = keep.tile([P, N // QUADRANT, QUADRANT], BF16, name="damp_turned", align_bytes=64)
+        damp_filled = keep.tile([P, N // QUADRANT, QUADRANT], BF16, name="damp_filled", align_bytes=64)
+        damp_all = keep.tile([P, N], BF16, name="damp_all", align_bytes=64)
+
+        for g in range(GROUPS):
+            prepare_first_tiles(g)
+            if g == 0:
+                nc.vector.transpose(damp_turned[:].rearrange("p b j -> p (b j)"), damp_rows[:])
+                nc.vector.tensor_copy(
+                    out=damp_filled[:], in_=damp_turned[:, :, 0:1].to_broadcast([P, N // QUADRANT, QUADRANT])
+                )
+            for m in range(FIRST_TILES):
+                anchor_pass(g, m)
+            prepare_syn(g)
+            if g == 0:
+                nc.vector.transpose(damp_all[:], damp_filled[:].rearrange("p b j -> p (b j)"))
+            for m in range(FIRST_TILES):
+                real_pass(g, m)
+            for m in range(FIRST_TILES):
+                syn_pass(g, m)
+
+        take_abs(0)
+        add_damp(0)
+        take_abs(1)
+
+        for m in range(FIRST_TILES, TILES):
+            prepare_tile(m)
+            if m == FIRST_TILES:
+                for g in range(GROUPS):
+                    anchor_pass(g, m)
+                    real_pass(g, m)
+                    syn_pass(g, m)
+            else:
                 anchor_passes(m)
-            if kind == "d":
+            if m >= ANCHOR_AHEAD_FROM:
+                diff_passes(m - 1)
+            epilogue_round(m - FIRST_TILES)
+            if FIRST_TILES < m < ANCHOR_AHEAD_FROM - 1:
                 diff_passes(m)
-            if kind == "r":
-                epilogue_round(m)
+        diff_passes(TILES - 1)
+        for r in range(TILES - FIRST_TILES, TILES + 1):
+            epilogue_round(r)

from contextlib import ExitStack

import concourse.mybir as mybir

S, F, N = 2048, 1536, 512
FLOPS = 3 * 2 * S * F * N

F32 = mybir.dt.float32
BF16 = mybir.dt.bfloat16
U32 = mybir.dt.uint32
I32 = mybir.dt.int32
U8 = mybir.dt.uint8
FP8X4 = mybir.dt.float8_e4m3fn_x4
FP4X4 = mybir.dt.float4_e2m1fn_x4
ALU = mybir.AluOpType
ACT = mybir.ActivationFunctionType

P = 128
PACK = 4
QUADRANT = 32
SCALE_ROWS = 4
GROUPS = S // (P * PACK)
TILES = F // P
BANKS = 8
FIRST_TILES = BANKS // 2
PAIR = 2
RUN = 4
SYN_VECTOR_COLUMNS = 320
ANCHOR_AHEAD_FROM = TILES - 2
WORD_BUFS = 8
DIVISOR_BUFS = 6
RESULT_BUFS = 6


def tile_label_distillation_discrepancy_s10_kernel(
    tc, acts, real_words, real_scales, anchor_words, anchor_scales, e_syn, damp, out
):
    nc = tc.nc
    with ExitStack() as ctx:
        keep = ctx.enter_context(tc.tile_pool(name="keep", bufs=1))
        stage = ctx.enter_context(tc.tile_pool(name="stage", bufs=1))
        psum = ctx.enter_context(tc.psum_pool(name="psum", bufs=1))
        ctx.enter_context(tc.manual_schedule())

        a_rows, syn_rows, anchor_codes, real_codes = {}, {}, {}, {}

        def load_rows(name, matrix, g, c0, c1):
            rows = keep.tile([P, PACK, c1 - c0], BF16, name=name)
            src = matrix[g * P * PACK : (g + 1) * P * PACK, c0:c1]
            nc.sync.dma_start(out=rows[:], in_=src.rearrange("(p t) c -> p t c", t=PACK))
            return rows

        def load_a(g, m0, m1):
            rows = load_rows("a_rows_%d_%d" % (g, m0), acts, g, m0 * P, m1 * P)
            for m in range(m0, m1):
                a_rows[g, m] = rows[:, :, (m - m0) * P : (m - m0 + 1) * P]

        def load_syn(g):
            syn_rows[g] = load_rows("syn_rows_%d" % g, e_syn, g, 0, N)

        def load_anchor(g):
            codes = keep.tile([P, N], U32, name="anchor_codes_%d" % g, align_bytes=64)
            src = anchor_words[g].rearrange("p n t -> p (n t)")
            nc.sync.dma_start(out=codes[:].bitcast(I32), in_=src.bitcast(I32))
            anchor_codes[g] = codes

        def load_real(g):
            codes = keep.tile([P, 2 * N], U8, name="real_codes_%d" % g, align_bytes=64)
            nc.sync.dma_start(out=codes[:].bitcast(I32), in_=real_words[g].bitcast(I32))
            real_codes[g] = codes

        damp_rows = keep.tile([P, N], BF16, name="damp_rows", align_bytes=64)
        nc.vector.memset(damp_rows[:].bitcast(I32), 0)
        nc.scalar.dma_start(out=damp_rows[0:P:QUADRANT, :], in_=damp.partition_broadcast(P // QUADRANT))

        anchor_plane = keep.tile([P, N], U8, name="anchor_plane", align_bytes=64)
        real_plane = keep.tile([P, GROUPS, N], U8, name="real_plane", align_bytes=64)
        nc.vector.memset(anchor_plane[:].bitcast(I32), 0)
        nc.vector.memset(real_plane[:].bitcast(I32), 0)

        def load_anchor_scales():
            for q in range(P // QUADRANT):
                nc.sync.dma_start(
                    out=anchor_plane[QUADRANT * q : QUADRANT * q + GROUPS * SCALE_ROWS, :].bitcast(I32),
                    in_=anchor_scales[:, SCALE_ROWS * q : SCALE_ROWS * (q + 1), :].bitcast(I32),
                )

        def load_real_scales():
            for q in range(P // QUADRANT):
                src = real_scales[:, SCALE_ROWS * q : SCALE_ROWS * (q + 1), :].rearrange("g r n -> r g n")
                nc.sync.dma_start(
                    out=real_plane[QUADRANT * q : QUADRANT * q + SCALE_ROWS].bitcast(I32), in_=src.bitcast(I32)
                )

        table_preload = keep.tile([P, 1], F32, name="table_preload")
        nc.vector.memset(table_preload[:], 1.0)
        nc.scalar.activation(out=table_preload[:], in_=table_preload[:], func=ACT.Abs_reciprocal_sqrt)

        load_a(0, 0, FIRST_TILES)
        load_anchor_scales()
        load_anchor(0)
        load_real(0)
        load_syn(0)
        load_real_scales()
        for g in range(1, GROUPS):
            load_a(g, 0, FIRST_TILES)
            load_anchor(g)
            load_syn(g)
            load_real(g)
        for m in range(FIRST_TILES, TILES, PAIR):
            for g in range(GROUPS):
                load_a(g, m, m + PAIR)

        def interleave_views(words, rows):
            return (
                words.rearrange("p (c i) t -> p c t i", i=RUN),
                rows.rearrange("p t (c i) -> p c t i", i=RUN),
            )

        a_words, a_codes, a_scales = {}, {}, {}

        def interleave_a(copy, g, m):
            words = stage.tile([P, P, PACK], BF16, name="a_words", bufs=WORD_BUFS, align_bytes=64)
            dst, src = interleave_views(words[:], a_rows[g, m])
            copy(out=dst, in_=src)
            a_words[g, m] = words

        def quantize_a(g, m):
            codes = keep.tile([P, P], U32, name="a_codes_%d_%d" % (g, m), align_bytes=64)
            scales = keep.tile([P, P], U8, name="a_scales_%d_%d" % (g, m), align_bytes=64)
            nc.vector.quantize_mx(
                out=codes[:].bitcast(FP8X4), scales=scales[:], in_=a_words[g, m][:].rearrange("p c t -> p (c t)")
            )
            a_codes[g, m], a_scales[g, m] = codes, scales

        on_vector, on_scalar = nc.vector.tensor_copy, nc.scalar.copy

        def prepare_first_tiles(g):
            for m in range(0, FIRST_TILES, 2):
                interleave_a(on_vector, g, m)
                interleave_a(on_scalar, g, m + 1)
            for m in list(range(0, FIRST_TILES, 2)) + list(range(1, FIRST_TILES, 2)):
                quantize_a(g, m)

        def prepare_tile(m):
            still_arriving = m == FIRST_TILES
            interleave_a(on_scalar, 0, m)
            interleave_a(on_vector, 1, m)
            if m % 2 == 1:
                interleave_a(on_scalar, 3, m)
            if still_arriving:
                quantize_a(0, m)
            interleave_a(on_vector, 2, m)
            if not still_arriving:
                quantize_a(0, m)
            quantize_a(1, m)
            if m % 2 == 0:
                interleave_a(on_vector, 3, m)
            quantize_a(2, m)
            quantize_a(3, m)

        syn_codes, syn_scales = {}, {}

        def prepare_syn(g):
            words = stage.tile([P, N, PACK], BF16, name="syn_words", bufs=2, align_bytes=64)
            dst, src = interleave_views(words[:, SYN_VECTOR_COLUMNS:, :], syn_rows[g][:, :, SYN_VECTOR_COLUMNS:])
            nc.scalar.activation(out=dst, in_=src, func=ACT.Copy, scale=-1.0)
            dst, src = interleave_views(words[:, :SYN_VECTOR_COLUMNS, :], syn_rows[g][:, :, :SYN_VECTOR_COLUMNS])
            nc.vector.tensor_scalar(out=dst, in0=src, scalar1=-1.0, scalar2=None, op0=ALU.mult)
            codes = keep.tile([P, N], U32, name="syn_codes_%d" % g, align_bytes=64)
            scales = keep.tile([P, N], U8, name="syn_scales_%d" % g, align_bytes=64)
            for cols in (slice(0, N // 2), slice(N // 2, N)):
                nc.vector.quantize_mx(
                    out=codes[:, cols].bitcast(FP8X4),
                    scales=scales[:, cols],
                    in_=words[:, cols, :].rearrange("p c t -> p (c t)"),
                )
            syn_codes[g], syn_scales[g] = codes, scales

        free_banks = ["bank_%d" % b for b in range(BANKS)]
        anchor_sum, anchor_bank, diff_sum, diff_bank = {}, {}, {}, {}

        def mx_pass(acc, g, m, codes, scales, start, stop):
            nc.tensor.matmul_mx(
                out=acc[:],
                lhsT=a_codes[g, m][:].bitcast(FP8X4),
                lhsT_scale=a_scales[g, m][:],
                rhs=codes,
                rhs_scale=scales,
                start=start,
                stop=stop,
            )

        def anchor_pass(g, m):
            if g == 0:
                anchor_bank[m] = free_banks.pop(0)
                anchor_sum[m] = psum.tile([P, N], F32, name=anchor_bank[m])
            codes, scales = anchor_codes[g][:].bitcast(FP8X4), anchor_plane[SCALE_ROWS * g :, :]
            mx_pass(anchor_sum[m], g, m, codes, scales, g == 0, g == GROUPS - 1)

        def real_pass(g, m):
            if g == 0:
                diff_bank[m] = free_banks.pop(0)
                diff_sum[m] = psum.tile([P, N], F32, name=diff_bank[m])
            mx_pass(diff_sum[m], g, m, real_codes[g][:].bitcast(FP4X4), real_plane[:, g, :], g == 0, False)

        def syn_pass(g, m):
            mx_pass(diff_sum[m], g, m, syn_codes[g][:].bitcast(FP8X4), syn_scales[g][:], False, g == GROUPS - 1)

        def anchor_passes(m):
            for g in range(GROUPS):
                anchor_pass(g, m)

        def diff_passes(m):
            for g in range(GROUPS):
                real_pass(g, m)
            for g in range(GROUPS):
                syn_pass(g, m)

        divisor = {}

        def take_abs(m):
            divisor[m] = stage.tile([P, N], F32, name="divisor", bufs=DIVISOR_BUFS)
            nc.scalar.activation(out=divisor[m][:], in_=anchor_sum[m][:], func=ACT.Abs)
            free_banks.append(anchor_bank[m])

        def add_damp(m):
            nc.vector.tensor_tensor(out=divisor[m][:], in0=divisor[m][:], in1=damp_all[:], op=ALU.add)

        def inverse_root(m):
            nc.scalar.activation(out=divisor[m][:], in_=divisor[m][:], func=ACT.Abs_reciprocal_sqrt)

        def square(m):
            nc.scalar.activation(out=divisor[m][:], in_=divisor[m][:], func=ACT.Square)

        def multiply_and_store(m):
            result = stage.tile([P, N], F32, name="result", bufs=RESULT_BUFS)
            pieces = 2 if m == TILES - 1 else 1
            for h in range(pieces):
                cols = slice(h * N // pieces, (h + 1) * N // pieces)
                nc.vector.tensor_tensor(
                    out=result[:, cols], in0=diff_sum[m][:, cols], in1=divisor[m][:, cols], op=ALU.mult
                )
                nc.sync.dma_start(out=out[m * P : (m + 1) * P, cols], in_=result[:, cols])
            free_banks.append(diff_bank[m])

        def epilogue_round(r):
            if r < TILES:
                inverse_root(r)
            if r + 2 < TILES:
                take_abs(r + 2)
            if r < TILES:
                square(r)
            if r > 0:
                multiply_and_store(r - 1)
            if r + 1 < TILES:
                add_damp(r + 1)

        damp_turned = keep.tile([P, N // QUADRANT, QUADRANT], BF16, name="damp_turned", align_bytes=64)
        damp_filled = keep.tile([P, N // QUADRANT, QUADRANT], BF16, name="damp_filled", align_bytes=64)
        damp_all = keep.tile([P, N], BF16, name="damp_all", align_bytes=64)

        for g in range(GROUPS):
            prepare_first_tiles(g)
            if g == 0:
                nc.vector.transpose(damp_turned[:].rearrange("p b j -> p (b j)"), damp_rows[:])
                nc.vector.tensor_copy(
                    out=damp_filled[:], in_=damp_turned[:, :, 0:1].to_broadcast([P, N // QUADRANT, QUADRANT])
                )
            for m in range(FIRST_TILES):
                anchor_pass(g, m)
            prepare_syn(g)
            if g == 0:
                nc.vector.transpose(damp_all[:], damp_filled[:].rearrange("p b j -> p (b j)"))
            for m in range(FIRST_TILES):
                real_pass(g, m)
            for m in range(FIRST_TILES):
                syn_pass(g, m)

        take_abs(0)
        add_damp(0)
        take_abs(1)

        for m in range(FIRST_TILES, TILES):
            prepare_tile(m)
            if m == FIRST_TILES:
                for g in range(GROUPS):
                    anchor_pass(g, m)
                    real_pass(g, m)
                    syn_pass(g, m)
            else:
                anchor_passes(m)
            if m >= ANCHOR_AHEAD_FROM:
                diff_passes(m - 1)
            epilogue_round(m - FIRST_TILES)
            if FIRST_TILES < m < ANCHOR_AHEAD_FROM - 1:
                diff_passes(m)
        diff_passes(TILES - 1)
        for r in range(TILES - FIRST_TILES, TILES + 1):
            epilogue_round(r)
